import numpy as np
import ml_dtypes


def mxq(x, axis, fmt="e4m3"):
    dtype, down = {"e4m3": (ml_dtypes.float8_e4m3fn, 7), "e5m2": (ml_dtypes.float8_e5m2, 14)}[fmt]
    v = np.moveaxis(np.asarray(x, np.float32).astype(ml_dtypes.bfloat16).astype(np.float64), axis, -1)
    blocks = v.reshape(v.shape[:-1] + (-1, 32))
    amax = np.abs(blocks).max(-1, keepdims=True)
    byte = np.maximum(np.where(amax > 0, np.frexp(amax)[1] - 1 + 127, 0) - down, 1)
    scale = np.exp2(byte - 127.0)
    codes = (blocks / scale).astype(np.float32).astype(dtype).astype(np.float64)
    return np.moveaxis((codes * scale).reshape(v.shape), -1, axis)


WIDE = False


def mx_kscale(k):
    if not WIDE:
        return np.ones(k)
    levels = np.array([10, -10, 5, -5, 0])
    if k % 512:
        return np.exp2(np.random.permutation(np.resize(levels, k // 32))).repeat(32)
    a = np.empty((k // 512, 16))
    for p in range(k // 512):
        a[p, :8] = np.random.permutation(np.resize(levels, 8))
        for g in range(8):
            far = levels[np.abs(levels - a[p, g]) >= 10]
            a[p, g + 8] = far[np.random.randint(len(far))]
    return np.exp2(a.ravel()).repeat(32)


def f64(x):
    return np.asarray(x).astype(np.float64)


def striped8(idx):
    return np.asarray(idx).reshape(8, -1, 16).transpose(0, 2, 1).reshape(128, -1).astype(np.uint16)


def unstriped8(offs):
    return offs.reshape(8, 16, -1).transpose(0, 2, 1).reshape(8, -1).astype(np.int64)


def pick8(x, idx, run):
    r = np.arange(len(x))
    return x[r[:, None], idx[r % (8 * run) // run]]


D, T, I, Q, X, E, F = 512, 2048, 512, 256, 32, 512, 512


def setup_inputs():
    n = np.random.standard_normal
    idx = np.stack([np.random.permutation(T)[:I] for _ in range(8)])
    fd = mx_kscale(D)
    fi = mx_kscale(I)
    fe = mx_kscale(E)
    ti = np.ones((8, T))
    np.put_along_axis(ti, idx, np.tile(fi, (8, 1)), axis=1)
    return {
        "query": (n((D, Q)) * (np.arange(D)[:, None] // 64 == np.arange(Q) % 8) * 0.1 * fd[:, None]).astype(np.float32),
        "keys": (n((D, T)) / fd[:, None]).astype(np.float32),
        "size": (np.random.uniform(8.0, 24.0, (1, I)) * fi).astype(np.float32),
        "vals": (n((E, T)) / ti[np.arange(E) % 512 // 64]).astype(np.float32),
        "own": ((np.arange(E)[:, None] // 64 == np.arange(Q) % 8) * 1.0).astype(np.float32),
        "esc": (np.random.uniform(0.5, 2.0, (E, 1)) * fe[:, None]).astype(np.float32),
        "wo": (n((E, F)) * 1 / np.sqrt(E) / fe[:, None]).astype(np.float32),
        "res": (n((F, X)) * 1.5).astype(np.float32),
        "offs": striped8(idx),
    }


def reference(query, keys, size, vals, own, esc, wo, res, offs):
    idx = unstriped8(offs)
    queryq = mxq(f64(query), 0, "e4m3")
    keysidxq = mxq(pick8(f64(keys), idx, 64), 0, "e4m3")
    a = queryq.T @ keysidxq
    p = np.exp(a - np.max(a, axis=1, keepdims=True))
    w = p * f64(size) / np.sum(p, axis=1, keepdims=True)
    wt = w.T
    vt = pick8(f64(vals), idx, 64).T
    vtq = mxq(vt, 0, "e4m3")
    wtq = mxq(wt, 0, "e4m3")
    o = vtq.T @ wtq
    ob = o * f64(own) * f64(esc)
    woq = mxq(f64(wo), 0, "e4m3")
    obq = mxq(ob, 0, "e4m3")
    z = woq.T @ obq
    y = z.reshape(F, X, Q // X).sum(axis=2) + f64(res)
    return y

@@ -1,0 +1,197 @@
+from contextlib import ExitStack
+
+import concourse.mybir as mybir
+from concourse.masks import make_identity
+
+D, T, I, Q, X, E, F = 512, 2048, 512, 256, 32, 512, 512
+FLOPS = 2 * Q * I * D + 2 * E * Q * I + 2 * F * Q * E
+
+F32 = mybir.dt.float32
+BF16 = mybir.dt.bfloat16
+U32 = mybir.dt.uint32
+U16 = mybir.dt.uint16
+U8 = mybir.dt.uint8
+FP8X4 = mybir.dt.float8_e4m3fn_x4
+ALU = mybir.AluOpType
+ACT = mybir.ActivationFunctionType
+AX = mybir.AxisListType
+
+P = 128
+PACK = 4
+
+
+def quantize(nc, codes, scales, values):
+    nc.vector.quantize_mx(out=codes.bitcast(FP8X4), scales=scales, in_=values)
+
+
+def mx_pass(nc, out, lhs, rhs, start=True, stop=True):
+    nc.tensor.matmul_mx(
+        out=out,
+        lhsT=lhs[0].bitcast(FP8X4),
+        lhsT_scale=lhs[1],
+        rhs=rhs[0].bitcast(FP8X4),
+        rhs_scale=rhs[1],
+        start=start,
+        stop=stop,
+    )
+
+
+def tile_attend_ownlists_project_kernel(tc, query, keys, size, vals, own, esc, wo, res, offs, out):
+    nc = tc.nc
+    with ExitStack() as ctx:
+        sb = ctx.enter_context(tc.tile_pool(name="sb", bufs=1))
+        ps = ctx.enter_context(tc.psum_pool(name="ps", bufs=1))
+
+        def mx_tiles(name, width):
+            codes = sb.tile([P, width], U32, name=name + "_codes", align_bytes=64)
+            scales = sb.tile([P, width], U8, name=name + "_scales", align_bytes=64)
+            return codes, scales
+
+        lists = sb.tile([P, I // 16], U16, name="lists")
+        key_planes = keys.rearrange("(p t) n -> t p n", t=PACK)
+        val_planes = vals.rearrange("(p t) n -> t p n", t=PACK)
+        key_pool = [sb.tile([P, T], F32, name="key_pool%d" % t) for t in range(PACK)]
+        val_pool = [sb.tile([P, T], F32, name="val_pool%d" % t) for t in range(PACK)]
+        q_raw = sb.tile([P, PACK, Q], F32, name="q_raw")
+        own_sb = sb.tile([P, PACK, Q], F32, name="own_sb")
+        wo_raw = [sb.tile([P, PACK, F // 2], F32, name="wo_raw%d" % h) for h in range(2)]
+        size_sb = sb.tile([P, PACK], F32, name="size_sb")
+        esc_sb = sb.tile([P, PACK], F32, name="esc_sb")
+        res_sb = sb.tile([P, 2, 2 * X], F32, name="res_sb")
+
+        nc.sync.dma_start(out=key_pool[0][:], in_=key_planes[0])
+        nc.sync.dma_start(lists[:], offs)
+        nc.scalar.dma_start(out=size_sb[:], in_=size.rearrange("o (p t) -> p (o t)", t=PACK))
+        nc.scalar.dma_start(out=esc_sb[:], in_=esc.rearrange("(p t) o -> p (t o)", t=PACK))
+        nc.scalar.dma_start(out=res_sb[:], in_=res.rearrange("(h p c) x -> p h (c x)", h=2, c=2))
+        nc.sync.dma_start(out=q_raw[:], in_=query.rearrange("(p t) q -> p t q", t=PACK))
+        for t in range(1, PACK):
+            nc.sync.dma_start(out=key_pool[t][:], in_=key_planes[t])
+        for t in range(PACK):
+            nc.sync.dma_start(out=val_pool[t][:], in_=val_planes[t])
+        nc.sync.dma_start(out=own_sb[:], in_=own.rearrange("(p t) q -> p t q", t=PACK))
+        wo_rows = wo.rearrange("(p t) f -> p t f", t=PACK)
+        for h in range(2):
+            nc.sync.dma_start(out=wo_raw[h][:], in_=wo_rows[:, :, h * (F // 2) : (h + 1) * (F // 2)])
+
+        ident = sb.tile([P, P], F32, name="ident")
+        make_identity(nc, ident[:])
+
+        size_ps = ps.tile([P, PACK, P], F32, name="size_ps")
+        for t in range(PACK):
+            nc.tensor.transpose(size_ps[:, t, :], size_sb[:, t : t + 1].to_broadcast([P, P]), ident[:])
+
+        q_bf = sb.tile([P, Q * PACK], BF16, name="q_bf", align_bytes=64)
+        nc.scalar.copy(
+            out=q_bf[:].rearrange("p (c i t) -> p c t i", i=4, t=PACK),
+            in_=q_raw[:].rearrange("p t (c i) -> p c t i", i=4),
+        )
+        q_mx = mx_tiles("q", Q)
+        quantize(nc, q_mx[0][:], q_mx[1][:], q_bf[:])
+
+        k_got = sb.tile([P, PACK, I], BF16, name="k_got")
+        for t in range(PACK):
+            nc.vector.tensor_copy(k_got[:, t, :], key_pool[t][:].indirect(lists[:]))
+        k_bf = sb.tile([P, I * PACK], BF16, name="k_bf", align_bytes=64)
+        nc.vector.tensor_copy(
+            out=k_bf[:].rearrange("p (c i t) -> p c t i", i=4, t=PACK),
+            in_=k_got[:].rearrange("p t (c i) -> p c t i", i=4),
+        )
+        k_mx = mx_tiles("k", I)
+        quantize(nc, k_mx[0][:], k_mx[1][:], k_bf[:])
+
+        wt_ps = ps.tile([P, 2, 2, P], F32, name="wt_ps")
+        wt_bf = sb.tile([P, Q * PACK], BF16, name="wt_bf", align_bytes=64)
+        for g in range(2):
+            cols = slice(g * P, (g + 1) * P)
+            score = ps.tile([P, I], F32, name="score%d" % g, tag="score%d" % g)
+            mx_pass(nc, score[:], (q_mx[0][:, cols], q_mx[1][:, cols]), (k_mx[0][:], k_mx[1][:]))
+            neg_max = sb.tile([P, 1], F32, name="neg_max%d" % g)
+            nc.vector.tensor_reduce(neg_max[:], score[:], AX.X, ALU.max, negate=True)
+            prob = sb.tile([P, I], F32, name="prob%d" % g)
+            total = sb.tile([P, 1], F32, name="total%d" % g)
+            nc.scalar.activation(prob[:], score[:], ACT.Exp, bias=neg_max[:], scale=1.0, accum_out=total[:])
+            inv = sb.tile([P, 1], F32, name="inv%d" % g)
+            nc.vector.reciprocal(inv[:], total[:])
+            w_bf = sb.tile([P, I], BF16, name="w_bf%d" % g)
+            nc.vector.scalar_tensor_tensor(
+                w_bf[:].rearrange("p (s t) -> p s t", t=PACK),
+                prob[:].rearrange("p (s t) -> p s t", t=PACK),
+                inv[:],
+                size_ps[:].rearrange("p t s -> p s t"),
+                ALU.mult,
+                ALU.mult,
+            )
+            words = w_bf[:].bitcast(F32)
+            for u in range(2):
+                nc.tensor.transpose(wt_ps[:, g, u, :], words[:, u : I // 2 : 2], ident[:])
+        nc.scalar.copy(
+            out=wt_bf[:].bitcast(F32).rearrange("p (g q u) -> p g q u", g=2, u=2),
+            in_=wt_ps[:].rearrange("p g u q -> p g q u"),
+        )
+        wt_mx = mx_tiles("wt", Q)
+        quantize(nc, wt_mx[0][:], wt_mx[1][:], wt_bf[:])
+
+        ob_rows = sb.tile([P, PACK, Q], BF16, name="ob_rows")
+        o_ps = [ps.tile([P, 2, Q], F32, name="o_ps%d" % b) for b in range(2)]
+        for t in range(PACK):
+            v_got = sb.tile([P, I], BF16, name="v_got%d" % t)
+            nc.vector.tensor_copy(v_got[:], val_pool[t][:].indirect(lists[:]))
+            vt_ps = ps.tile([P, 2, P], F32, name="vt_ps%d" % t, tag="vt_ps%d" % (t % 2))
+            words = v_got[:].bitcast(F32)
+            for u in range(2):
+                nc.tensor.transpose(vt_ps[:, u, :], words[:, u : I // 2 : 2], ident[:])
+            vt_bf = sb.tile([P, P * PACK], BF16, name="vt_bf%d" % t, align_bytes=64)
+            nc.scalar.copy(
+                out=vt_bf[:].bitcast(F32).rearrange("p (e u) -> p e u", u=2),
+                in_=vt_ps[:].rearrange("p u e -> p e u"),
+            )
+            vt_mx = mx_tiles("vt%d" % t, P)
+            quantize(nc, vt_mx[0][:], vt_mx[1][:], vt_bf[:])
+            o_t = o_ps[t // 2][:, t % 2, :]
+            mx_pass(nc, o_t, (vt_mx[0][:], vt_mx[1][:]), (wt_mx[0][:], wt_mx[1][:]))
+            nc.vector.scalar_tensor_tensor(
+                ob_rows[:, t, :], o_t, esc_sb[:, t : t + 1], own_sb[:, t, :], ALU.mult, ALU.mult
+            )
+
+        ob_mx = []
+        ob_half = []
+        for u in range(2):
+            ob_bf = sb.tile([P, P * PACK], BF16, name="ob_bf%d" % u, align_bytes=64)
+            nc.vector.tensor_copy(
+                out=ob_bf[:].rearrange("p (x j t) -> p x t j", j=4, t=PACK),
+                in_=ob_rows[:].rearrange("p t (x u j) -> p u x t j", u=2, j=4)[:, u],
+            )
+            ob_half.append(ob_bf)
+        for u in range(2):
+            pair = mx_tiles("ob%d" % u, P)
+            quantize(nc, pair[0][:], pair[1][:], ob_half[u][:])
+            ob_mx.append(pair)
+
+        z_ps = ps.tile([P, PACK, P], F32, name="z_ps", tag="score0")
+        for h in range(2):
+            wo_bf = sb.tile([P, (F // 2) * PACK], BF16, name="wo_bf%d" % h, align_bytes=64)
+            nc.scalar.copy(
+                out=wo_bf[:].rearrange("p (c m i t) -> p c m t i", c=2, i=2, t=PACK),
+                in_=wo_raw[h][:].rearrange("p t (m i c) -> p c m t i", i=2, c=2),
+            )
+            wo_mx = mx_tiles("wo%d" % h, F // 2)
+            quantize(nc, wo_mx[0][:], wo_mx[1][:], wo_bf[:])
+            for c in range(2):
+                cols = slice(c * P, (c + 1) * P)
+                for u in range(2):
+                    mx_pass(
+                        nc,
+                        z_ps[:, 2 * h + c, :],
+                        (wo_mx[0][:, cols], wo_mx[1][:, cols]),
+                        (ob_mx[u][0][:], ob_mx[u][1][:]),
+                        start=(u == 0),
+                        stop=(u == 1),
+                    )
+        z_sum = sb.tile([P, PACK * X], F32, name="z_sum")
+        nc.vector.tensor_reduce(z_sum[:], z_ps[:].rearrange("p c (x j) -> p (c x) j", j=4), AX.X, ALU.add)
+        y = sb.tile([P, 2, 2 * X], F32, name="y")
+        nc.vector.tensor_tensor(
+            y[:].rearrange("p h n -> p (h n)"), z_sum[:], res_sb[:].rearrange("p h n -> p (h n)"), ALU.add
+        )
+        nc.sync.dma_start(out=out.rearrange("(h p c) x -> p h (c x)", h=2, c=2), in_=y[:])

@@ -42,8 +42,8 @@ def tile_attend_ownlists_project_kernel(tc, query, keys, size, vals, own, esc, w
         sb = ctx.enter_context(tc.tile_pool(name="sb", bufs=1))
         ps = ctx.enter_context(tc.psum_pool(name="ps", bufs=1))
 
-        def mx_tiles(name, width):
-            codes = sb.tile([P, width], U32, name=name + "_codes", align_bytes=64)
+        def mx_tiles(name, width, tag=None):
+            codes = sb.tile([P, width], U32, name=name + "_codes", tag=tag or name + "_codes", align_bytes=64)
             scales = sb.tile([P, width], U8, name=name + "_scales", align_bytes=64)
             return codes, scales
 
@@ -51,7 +51,9 @@ def tile_attend_ownlists_project_kernel(tc, query, keys, size, vals, own, esc, w
         key_planes = keys.rearrange("(p t) n -> t p n", t=PACK)
         val_planes = vals.rearrange("(p t) n -> t p n", t=PACK)
         key_pool = [sb.tile([P, T], F32, name="key_pool%d" % t) for t in range(PACK)]
-        val_pool = [sb.tile([P, T], F32, name="val_pool%d" % t) for t in range(PACK)]
+        val_pool = [
+            sb.tile([P, T], F32, name="val_pool%d" % t, tag="val_pool%d" % t, align_bytes=64) for t in range(PACK)
+        ]
         q_raw = sb.tile([P, PACK, Q], F32, name="q_raw")
         own_sb = sb.tile([P, PACK, Q], F32, name="own_sb")
         wo_raw = [sb.tile([P, PACK, F // 2], F32, name="wo_raw%d" % h) for h in range(2)]
@@ -64,9 +66,9 @@ def tile_attend_ownlists_project_kernel(tc, query, keys, size, vals, own, esc, w
         nc.scalar.dma_start(out=size_sb[:], in_=size.rearrange("o (p t) -> p (o t)", t=PACK))
         nc.scalar.dma_start(out=esc_sb[:], in_=esc.rearrange("(p t) o -> p (t o)", t=PACK))
         nc.scalar.dma_start(out=res_sb[:], in_=res.rearrange("(h p c) x -> p h (c x)", h=2, c=2))
-        nc.sync.dma_start(out=q_raw[:], in_=query.rearrange("(p t) q -> p t q", t=PACK))
         for t in range(1, PACK):
             nc.sync.dma_start(out=key_pool[t][:], in_=key_planes[t])
+        nc.sync.dma_start(out=q_raw[:], in_=query.rearrange("(p t) q -> p t q", t=PACK))
         for t in range(PACK):
             nc.sync.dma_start(out=val_pool[t][:], in_=val_planes[t])
         nc.sync.dma_start(out=own_sb[:], in_=own.rearrange("(p t) q -> p t q", t=PACK))
@@ -77,41 +79,66 @@ def tile_attend_ownlists_project_kernel(tc, query, keys, size, vals, own, esc, w
         ident = sb.tile([P, P], F32, name="ident")
         make_identity(nc, ident[:])
 
-        size_ps = ps.tile([P, PACK, P], F32, name="size_ps")
+        size_ps = ps.tile([P, PACK, P], F32, name="size_ps", tag="size_ps")
         for t in range(PACK):
             nc.tensor.transpose(size_ps[:, t, :], size_sb[:, t : t + 1].to_broadcast([P, P]), ident[:])
 
-        q_bf = sb.tile([P, Q * PACK], BF16, name="q_bf", align_bytes=64)
+        q_bf = sb.tile([P, Q * PACK], BF16, name="q_bf", tag="q_bf", align_bytes=64)
         nc.scalar.copy(
-            out=q_bf[:].rearrange("p (c i t) -> p c t i", i=4, t=PACK),
-            in_=q_raw[:].rearrange("p t (c i) -> p c t i", i=4),
+            out=q_bf[:].rearrange("p (u x j t) -> p u x t j", u=2, j=4, t=PACK),
+            in_=q_raw[:].rearrange("p t (x u j) -> p u x t j", u=2, j=4),
         )
         q_mx = mx_tiles("q", Q)
         quantize(nc, q_mx[0][:], q_mx[1][:], q_bf[:])
 
-        k_got = sb.tile([P, PACK, I], BF16, name="k_got")
-        for t in range(PACK):
-            nc.vector.tensor_copy(k_got[:, t, :], key_pool[t][:].indirect(lists[:]))
         k_bf = sb.tile([P, I * PACK], BF16, name="k_bf", align_bytes=64)
-        nc.vector.tensor_copy(
-            out=k_bf[:].rearrange("p (c i t) -> p c t i", i=4, t=PACK),
-            in_=k_got[:].rearrange("p t (c i) -> p c t i", i=4),
-        )
+        k_places = k_bf[:].rearrange("p (c i u t) -> p u c t i", i=4, u=2, t=2)
+        for u in range(2):
+            k_got = sb.tile([P, 2, I], BF16, name="k_got%d" % u)
+            for t in range(2):
+                nc.vector.tensor_copy(k_got[:, t, :], key_pool[2 * u + t][:].indirect(lists[:]))
+            nc.vector.tensor_copy(out=k_places[:, u], in_=k_got[:].rearrange("p t (c i) -> p c t i", i=4))
         k_mx = mx_tiles("k", I)
         quantize(nc, k_mx[0][:], k_mx[1][:], k_bf[:])
 
-        wt_ps = ps.tile([P, 2, 2, P], F32, name="wt_ps")
-        wt_bf = sb.tile([P, Q * PACK], BF16, name="wt_bf", align_bytes=64)
+        v_got = []
+        for t in range(PACK):
+            got = sb.tile([P, I], BF16, name="v_got%d" % t)
+            if t == 0:
+                pool_bf = sb.tile([P, T], BF16, name="pool_bf")
+                nc.scalar.activation(pool_bf[:], val_pool[0][:], ACT.Copy)
+            else:
+                nc.vector.tensor_copy(got[:], val_pool[t][:].indirect(lists[:]))
+            v_got.append(got)
+
+        early_bf = sb.tile([P, 2 * Q * PACK], BF16, name="early_bf", align_bytes=64)
+
+        def turn(src, dst, name, bank):
+            turned = ps.tile([P, 2, P], F32, name="turned_" + name, tag="turn%d" % bank)
+            words = src.bitcast(F32)
+            for u in range(2):
+                nc.tensor.transpose(turned[:, u, :], words[:, u : I // 2 : 2], ident[:])
+            nc.scalar.copy(
+                out=dst.bitcast(F32).rearrange("p (e u) -> p e u", u=2),
+                in_=turned[:].rearrange("p u e -> p e u"),
+            )
+
+        probs = []
         for g in range(2):
             cols = slice(g * P, (g + 1) * P)
             score = ps.tile([P, I], F32, name="score%d" % g, tag="score%d" % g)
             mx_pass(nc, score[:], (q_mx[0][:, cols], q_mx[1][:, cols]), (k_mx[0][:], k_mx[1][:]))
-            neg_max = sb.tile([P, 1], F32, name="neg_max%d" % g)
+            neg_max = sb.tile([P, 1], F32, name="neg_max%d" % g, tag="neg_max%d" % g)
             nc.vector.tensor_reduce(neg_max[:], score[:], AX.X, ALU.max, negate=True)
             prob = sb.tile([P, I], F32, name="prob%d" % g)
             total = sb.tile([P, 1], F32, name="total%d" % g)
             nc.scalar.activation(prob[:], score[:], ACT.Exp, bias=neg_max[:], scale=1.0, accum_out=total[:])
-            inv = sb.tile([P, 1], F32, name="inv%d" % g)
+            probs.append((prob, total))
+        nc.scalar.activation(v_got[0][:], pool_bf[:].indirect(lists[:]), ACT.Copy)
+        turn(v_got[1][:], early_bf[:, 3 * I : 4 * I], "v1", 0)
+        for g in range(2):
+            prob, total = probs[g]
+            inv = sb.tile([P, 1], F32, name="inv%d" % g, tag=("val_pool1", "inv1")[g], align_bytes=64)
             nc.vector.reciprocal(inv[:], total[:])
             w_bf = sb.tile([P, I], BF16, name="w_bf%d" % g)
             nc.vector.scalar_tensor_tensor(
@@ -122,76 +149,65 @@ def tile_attend_ownlists_project_kernel(tc, query, keys, size, vals, own, esc, w
                 ALU.mult,
                 ALU.mult,
             )
-            words = w_bf[:].bitcast(F32)
-            for u in range(2):
-                nc.tensor.transpose(wt_ps[:, g, u, :], words[:, u : I // 2 : 2], ident[:])
-        nc.scalar.copy(
-            out=wt_bf[:].bitcast(F32).rearrange("p (g q u) -> p g q u", g=2, u=2),
-            in_=wt_ps[:].rearrange("p g u q -> p g q u"),
-        )
-        wt_mx = mx_tiles("wt", Q)
-        quantize(nc, wt_mx[0][:], wt_mx[1][:], wt_bf[:])
+            turn(w_bf[:], early_bf[:, g * I : (g + 1) * I], "w%d" % g, 1 + g)
+        turn(v_got[0][:], early_bf[:, 2 * I : 3 * I], "v0", 0)
 
-        ob_rows = sb.tile([P, PACK, Q], BF16, name="ob_rows")
-        o_ps = [ps.tile([P, 2, Q], F32, name="o_ps%d" % b) for b in range(2)]
+        early_mx = mx_tiles("early", 2 * Q, tag="val_pool3")
+        quantize(nc, early_mx[0][:], early_mx[1][:], early_bf[:])
+        vt_mx = [(early_mx[0][:, Q + t * P : Q + (t + 1) * P], early_mx[1][:, Q + t * P : Q + (t + 1) * P]) for t in range(2)]
+
+        factor = sb.tile([P, PACK, Q], F32, name="factor")
+        late_bf = sb.tile([P, 2 * I], BF16, name="late_bf", align_bytes=64)
+        for t in range(2):
+            turn(v_got[2 + t][:], late_bf[:, t * I : (t + 1) * I], "v%d" % (2 + t), 1 + t)
+        for r in range(PACK):
+            nc.vector.tensor_scalar_mul(factor[:, r, :], own_sb[:, r, :], esc_sb[:, r : r + 1])
+        late_mx = mx_tiles("late", 2 * P)
+        quantize(nc, late_mx[0][:], late_mx[1][:], late_bf[:])
+        vt_mx.extend((late_mx[0][:, t * P : (t + 1) * P], late_mx[1][:, t * P : (t + 1) * P]) for t in range(2))
+
+        o_ps = [ps.tile([P, PACK, P], F32, name="o_ps%d" % u) for u in range(2)]
         for t in range(PACK):
-            v_got = sb.tile([P, I], BF16, name="v_got%d" % t)
-            nc.vector.tensor_copy(v_got[:], val_pool[t][:].indirect(lists[:]))
-            vt_ps = ps.tile([P, 2, P], F32, name="vt_ps%d" % t, tag="vt_ps%d" % (t % 2))
-            words = v_got[:].bitcast(F32)
             for u in range(2):
-                nc.tensor.transpose(vt_ps[:, u, :], words[:, u : I // 2 : 2], ident[:])
-            vt_bf = sb.tile([P, P * PACK], BF16, name="vt_bf%d" % t, align_bytes=64)
-            nc.scalar.copy(
-                out=vt_bf[:].bitcast(F32).rearrange("p (e u) -> p e u", u=2),
-                in_=vt_ps[:].rearrange("p u e -> p e u"),
-            )
-            vt_mx = mx_tiles("vt%d" % t, P)
-            quantize(nc, vt_mx[0][:], vt_mx[1][:], vt_bf[:])
-            o_t = o_ps[t // 2][:, t % 2, :]
-            mx_pass(nc, o_t, (vt_mx[0][:], vt_mx[1][:]), (wt_mx[0][:], wt_mx[1][:]))
-            nc.vector.scalar_tensor_tensor(
-                ob_rows[:, t, :], o_t, esc_sb[:, t : t + 1], own_sb[:, t, :], ALU.mult, ALU.mult
-            )
-
-        ob_mx = []
-        ob_half = []
+                cols = slice(u * P, (u + 1) * P)
+                mx_pass(nc, o_ps[u][:, t, :], vt_mx[t], (early_mx[0][:, cols], early_mx[1][:, cols]))
+        ob_bf = sb.tile([P, 2, P * PACK], BF16, name="ob_bf", align_bytes=64)
         for u in range(2):
-            ob_bf = sb.tile([P, P * PACK], BF16, name="ob_bf%d" % u, align_bytes=64)
-            nc.vector.tensor_copy(
-                out=ob_bf[:].rearrange("p (x j t) -> p x t j", j=4, t=PACK),
-                in_=ob_rows[:].rearrange("p t (x u j) -> p u x t j", u=2, j=4)[:, u],
+            nc.vector.tensor_tensor(
+                ob_bf[:, u, :].rearrange("p (x j t) -> p x t j", j=4, t=PACK),
+                o_ps[u][:].rearrange("p t (x j) -> p x t j", j=4),
+                factor[:].rearrange("p t (x u j) -> p u x t j", u=2, j=4)[:, u],
+                ALU.mult,
             )
-            ob_half.append(ob_bf)
-        for u in range(2):
-            pair = mx_tiles("ob%d" % u, P)
-            quantize(nc, pair[0][:], pair[1][:], ob_half[u][:])
-            ob_mx.append(pair)
-
-        z_ps = ps.tile([P, PACK, P], F32, name="z_ps", tag="score0")
+        wo_mx = []
         for h in range(2):
-            wo_bf = sb.tile([P, (F // 2) * PACK], BF16, name="wo_bf%d" % h, align_bytes=64)
+            wo_bf = sb.tile([P, (F // 2) * PACK], BF16, name="wo_bf%d" % h, tag="wo_bf%d" % h, align_bytes=64)
             nc.scalar.copy(
                 out=wo_bf[:].rearrange("p (c m i t) -> p c m t i", c=2, i=2, t=PACK),
                 in_=wo_raw[h][:].rearrange("p t (m i c) -> p c m t i", i=2, c=2),
             )
-            wo_mx = mx_tiles("wo%d" % h, F // 2)
-            quantize(nc, wo_mx[0][:], wo_mx[1][:], wo_bf[:])
+            wo_mx.append(mx_tiles("wo%d" % h, F // 2))
+            quantize(nc, wo_mx[h][0][:], wo_mx[h][1][:], wo_bf[:])
+            if h == 0:
+                ob_mx = mx_tiles("ob", Q)
+                quantize(nc, ob_mx[0][:], ob_mx[1][:], ob_bf[:].rearrange("p u n -> p (u n)"))
+
+        z_sum = sb.tile([P, 2, 2 * X], F32, name="z_sum", tag="wo_bf1", align_bytes=64)
+        for h in range(2):
+            z_ps = ps.tile([P, 2, P], F32, name="z_ps%d" % h, tag="score%d" % h)
             for c in range(2):
                 cols = slice(c * P, (c + 1) * P)
                 for u in range(2):
+                    half = slice(u * P, (u + 1) * P)
                     mx_pass(
                         nc,
-                        z_ps[:, 2 * h + c, :],
-                        (wo_mx[0][:, cols], wo_mx[1][:, cols]),
-                        (ob_mx[u][0][:], ob_mx[u][1][:]),
+                        z_ps[:, c, :],
+                        (wo_mx[h][0][:, cols], wo_mx[h][1][:, cols]),
+                        (ob_mx[0][:, half], ob_mx[1][:, half]),
                         start=(u == 0),
                         stop=(u == 1),
                     )
-        z_sum = sb.tile([P, PACK * X], F32, name="z_sum")
-        nc.vector.tensor_reduce(z_sum[:], z_ps[:].rearrange("p c (x j) -> p (c x) j", j=4), AX.X, ALU.add)
+            nc.vector.tensor_reduce(z_sum[:, h, :], z_ps[:].rearrange("p c (x j) -> p (c x) j", j=4), AX.X, ALU.add)
         y = sb.tile([P, 2, 2 * X], F32, name="y")
-        nc.vector.tensor_tensor(
-            y[:].rearrange("p h n -> p (h n)"), z_sum[:], res_sb[:].rearrange("p h n -> p (h n)"), ALU.add
-        )
+        nc.vector.tensor_tensor(y[:], z_sum[:], res_sb[:], ALU.add)
         nc.sync.dma_start(out=out.rearrange("(h p c) x -> p h (c x)", h=2, c=2), in_=y[:])

@@ -18,6 +18,7 @@ AX = mybir.AxisListType
 
 P = 128
 PACK = 4
+CAST_FIRST = 1536
 
 
 def quantize(nc, codes, scales, values):
@@ -55,23 +56,25 @@ def tile_attend_ownlists_project_kernel(tc, query, keys, size, vals, own, esc, w
             sb.tile([P, T], F32, name="val_pool%d" % t, tag="val_pool%d" % t, align_bytes=64) for t in range(PACK)
         ]
         q_raw = sb.tile([P, PACK, Q], F32, name="q_raw")
-        own_sb = sb.tile([P, PACK, Q], F32, name="own_sb")
+        own_sb = [sb.tile([P, 2, Q], F32, name="own_sb%d" % h, tag="own_sb%d" % h, align_bytes=64) for h in range(2)]
         wo_raw = [sb.tile([P, PACK, F // 2], F32, name="wo_raw%d" % h) for h in range(2)]
         size_sb = sb.tile([P, PACK], F32, name="size_sb")
         esc_sb = sb.tile([P, PACK], F32, name="esc_sb")
-        res_sb = sb.tile([P, 2, 2 * X], F32, name="res_sb")
+        res_sb = sb.tile([P, PACK, X], F32, name="res_sb")
 
         nc.sync.dma_start(out=key_pool[0][:], in_=key_planes[0])
         nc.sync.dma_start(lists[:], offs)
         nc.scalar.dma_start(out=size_sb[:], in_=size.rearrange("o (p t) -> p (o t)", t=PACK))
         nc.scalar.dma_start(out=esc_sb[:], in_=esc.rearrange("(p t) o -> p (t o)", t=PACK))
-        nc.scalar.dma_start(out=res_sb[:], in_=res.rearrange("(h p c) x -> p h (c x)", h=2, c=2))
+        nc.scalar.dma_start(out=res_sb[:], in_=res.rearrange("(c p) x -> p c x", p=P))
         for t in range(1, PACK):
             nc.sync.dma_start(out=key_pool[t][:], in_=key_planes[t])
         nc.sync.dma_start(out=q_raw[:], in_=query.rearrange("(p t) q -> p t q", t=PACK))
         for t in range(PACK):
             nc.sync.dma_start(out=val_pool[t][:], in_=val_planes[t])
-        nc.sync.dma_start(out=own_sb[:], in_=own.rearrange("(p t) q -> p t q", t=PACK))
+        own_rows = own.rearrange("(p t) q -> p t q", t=PACK)
+        for h in range(2):
+            nc.sync.dma_start(out=own_sb[h][:], in_=own_rows[:, 2 * h : 2 * h + 2, :])
         wo_rows = wo.rearrange("(p t) f -> p t f", t=PACK)
         for h in range(2):
             nc.sync.dma_start(out=wo_raw[h][:], in_=wo_rows[:, :, h * (F // 2) : (h + 1) * (F // 2)])
@@ -83,13 +86,15 @@ def tile_attend_ownlists_project_kernel(tc, query, keys, size, vals, own, esc, w
         for t in range(PACK):
             nc.tensor.transpose(size_ps[:, t, :], size_sb[:, t : t + 1].to_broadcast([P, P]), ident[:])
 
-        q_bf = sb.tile([P, Q * PACK], BF16, name="q_bf", tag="q_bf", align_bytes=64)
-        nc.scalar.copy(
-            out=q_bf[:].rearrange("p (u x j t) -> p u x t j", u=2, j=4, t=PACK),
-            in_=q_raw[:].rearrange("p t (x u j) -> p u x t j", u=2, j=4),
-        )
         q_mx = mx_tiles("q", Q)
-        quantize(nc, q_mx[0][:], q_mx[1][:], q_bf[:])
+        for u in range(2):
+            half = slice(u * P, (u + 1) * P)
+            q_bf = sb.tile([P, P * PACK], BF16, name="q_bf%d" % u, align_bytes=64)
+            nc.scalar.copy(
+                out=q_bf[:].rearrange("p (x j t) -> p x t j", j=4, t=PACK),
+                in_=q_raw[:].rearrange("p t (x u j) -> p u x t j", u=2, j=4)[:, u],
+            )
+            quantize(nc, q_mx[0][:, half], q_mx[1][:, half], q_bf[:])
 
         k_bf = sb.tile([P, I * PACK], BF16, name="k_bf", align_bytes=64)
         k_places = k_bf[:].rearrange("p (c i u t) -> p u c t i", i=4, u=2, t=2)
@@ -101,28 +106,28 @@ def tile_attend_ownlists_project_kernel(tc, query, keys, size, vals, own, esc, w
         k_mx = mx_tiles("k", I)
         quantize(nc, k_mx[0][:], k_mx[1][:], k_bf[:])
 
-        v_got = []
+        v_got = {}
         for t in range(PACK):
-            got = sb.tile([P, I], BF16, name="v_got%d" % t)
             if t == 0:
                 pool_bf = sb.tile([P, T], BF16, name="pool_bf")
-                nc.scalar.activation(pool_bf[:], val_pool[0][:], ACT.Copy)
-            else:
-                nc.vector.tensor_copy(got[:], val_pool[t][:].indirect(lists[:]))
-            v_got.append(got)
+                nc.scalar.activation(pool_bf[:, :CAST_FIRST], val_pool[0][:, :CAST_FIRST], ACT.Copy)
 
-        early_bf = sb.tile([P, 2 * Q * PACK], BF16, name="early_bf", align_bytes=64)
+        early_bf = sb.tile([P, 2 * Q * PACK], BF16, name="early_bf", tag="early_bf", align_bytes=64)
+        vt1_bf = sb.tile([P, I], BF16, name="vt1_bf", align_bytes=64)
 
-        def turn(src, dst, name, bank):
-            turned = ps.tile([P, 2, P], F32, name="turned_" + name, tag="turn%d" % bank)
-            words = src.bitcast(F32)
-            for u in range(2):
-                nc.tensor.transpose(turned[:, u, :], words[:, u : I // 2 : 2], ident[:])
+        def turn(sources, dst, name, bank):
+            n = len(sources)
+            turned = ps.tile([P, n, 2, P], F32, name="turned_" + name, tag="turn%d" % bank)
+            for a in range(n):
+                words = sources[a].bitcast(F32)
+                for u in range(2):
+                    nc.tensor.transpose(turned[:, a, u, :], words[:, u : I // 2 : 2], ident[:])
             nc.scalar.copy(
-                out=dst.bitcast(F32).rearrange("p (e u) -> p e u", u=2),
-                in_=turned[:].rearrange("p u e -> p e u"),
+                out=dst.bitcast(F32).rearrange("p (a e u) -> p a e u", a=n, u=2),
+                in_=turned[:].rearrange("p a u e -> p a e u"),
             )
 
+        total = sb.tile([P, 2], F32, name="total")
         probs = []
         for g in range(2):
             cols = slice(g * P, (g + 1) * P)
@@ -130,84 +135,104 @@ def tile_attend_ownlists_project_kernel(tc, query, keys, size, vals, own, esc, w
             mx_pass(nc, score[:], (q_mx[0][:, cols], q_mx[1][:, cols]), (k_mx[0][:], k_mx[1][:]))
             neg_max = sb.tile([P, 1], F32, name="neg_max%d" % g, tag="neg_max%d" % g)
             nc.vector.tensor_reduce(neg_max[:], score[:], AX.X, ALU.max, negate=True)
-            prob = sb.tile([P, I], F32, name="prob%d" % g)
-            total = sb.tile([P, 1], F32, name="total%d" % g)
-            nc.scalar.activation(prob[:], score[:], ACT.Exp, bias=neg_max[:], scale=1.0, accum_out=total[:])
-            probs.append((prob, total))
-        nc.scalar.activation(v_got[0][:], pool_bf[:].indirect(lists[:]), ACT.Copy)
-        turn(v_got[1][:], early_bf[:, 3 * I : 4 * I], "v1", 0)
+            prob = sb.tile([P, I], F32, name="prob%d" % g, tag="prob%d" % g)
+            nc.scalar.activation(prob[:], score[:], ACT.Exp, bias=neg_max[:], scale=1.0, accum_out=total[:, g : g + 1])
+            probs.append(prob)
+        for t in range(1, PACK):
+            v_got[t] = sb.tile([P, I], BF16, name="v_got%d" % t)
+            nc.vector.tensor_copy(v_got[t][:], val_pool[t][:].indirect(lists[:]))
+        inv = sb.tile([P, 2], F32, name="inv", tag="val_pool1", align_bytes=64)
+        nc.vector.reciprocal(inv[:], total[:])
+        weights = []
         for g in range(2):
-            prob, total = probs[g]
-            inv = sb.tile([P, 1], F32, name="inv%d" % g, tag=("val_pool1", "inv1")[g], align_bytes=64)
-            nc.vector.reciprocal(inv[:], total[:])
+            prob = probs[g]
             w_bf = sb.tile([P, I], BF16, name="w_bf%d" % g)
             nc.vector.scalar_tensor_tensor(
                 w_bf[:].rearrange("p (s t) -> p s t", t=PACK),
                 prob[:].rearrange("p (s t) -> p s t", t=PACK),
-                inv[:],
+                inv[:, g : g + 1],
                 size_ps[:].rearrange("p t s -> p s t"),
                 ALU.mult,
                 ALU.mult,
             )
-            turn(w_bf[:], early_bf[:, g * I : (g + 1) * I], "w%d" % g, 1 + g)
-        turn(v_got[0][:], early_bf[:, 2 * I : 3 * I], "v0", 0)
+            weights.append(w_bf[:])
+        turn([v_got[1][:], weights[0]], early_bf[:, : 2 * I], "v1w0", 0)
+        nc.scalar.activation(pool_bf[:, CAST_FIRST:], val_pool[0][:, CAST_FIRST:], ACT.Copy)
+        v_got[0] = sb.tile([P, I], BF16, name="v_got0", tag="neg_max1")
+        nc.scalar.activation(v_got[0][:], pool_bf[:].indirect(lists[:]), ACT.Copy)
+        turn([v_got[0][:], weights[1]], early_bf[:, 2 * I :], "v0w1", 1)
 
-        early_mx = mx_tiles("early", 2 * Q, tag="val_pool3")
-        quantize(nc, early_mx[0][:], early_mx[1][:], early_bf[:])
-        vt_mx = [(early_mx[0][:, Q + t * P : Q + (t + 1) * P], early_mx[1][:, Q + t * P : Q + (t + 1) * P]) for t in range(2)]
-
+        early_mx = mx_tiles("early", 5 * P, tag="val_pool3")
+        quantize(nc, early_mx[0][:, : 4 * P], early_mx[1][:, : 4 * P], early_bf[:])
         factor = sb.tile([P, PACK, Q], F32, name="factor")
-        late_bf = sb.tile([P, 2 * I], BF16, name="late_bf", align_bytes=64)
-        for t in range(2):
-            turn(v_got[2 + t][:], late_bf[:, t * I : (t + 1) * I], "v%d" % (2 + t), 1 + t)
-        for r in range(PACK):
-            nc.vector.tensor_scalar_mul(factor[:, r, :], own_sb[:, r, :], esc_sb[:, r : r + 1])
-        late_mx = mx_tiles("late", 2 * P)
-        quantize(nc, late_mx[0][:], late_mx[1][:], late_bf[:])
-        vt_mx.extend((late_mx[0][:, t * P : (t + 1) * P], late_mx[1][:, t * P : (t + 1) * P]) for t in range(2))
+        turn([v_got[2][:]], vt1_bf[:], "v2", 2)
+        quantize(nc, early_mx[0][:, 4 * P :], early_mx[1][:, 4 * P :], vt1_bf[:])
+        for r in range(2):
+            nc.scalar.activation(factor[:, r, :], own_sb[0][:, r, :], ACT.Copy, scale=esc_sb[:, r : r + 1])
+            nc.vector.tensor_scalar_mul(factor[:, 2 + r, :], own_sb[1][:, r, :], esc_sb[:, 2 + r : 3 + r])
+        vt3_bf = sb.tile([P, I], BF16, name="vt3_bf", tag="own_sb0", align_bytes=64)
+        turn([v_got[3][:]], vt3_bf[:], "v3", 0)
+        vt3_mx = mx_tiles("vt3", P)
+        quantize(nc, vt3_mx[0][:], vt3_mx[1][:], vt3_bf[:])
+        vt_mx = [
+            (early_mx[0][:, 2 * P : 3 * P], early_mx[1][:, 2 * P : 3 * P]),
+            (early_mx[0][:, :P], early_mx[1][:, :P]),
+            (early_mx[0][:, 4 * P :], early_mx[1][:, 4 * P :]),
+            (vt3_mx[0][:], vt3_mx[1][:]),
+        ]
 
         o_ps = [ps.tile([P, PACK, P], F32, name="o_ps%d" % u) for u in range(2)]
-        for t in range(PACK):
-            for u in range(2):
-                cols = slice(u * P, (u + 1) * P)
-                mx_pass(nc, o_ps[u][:, t, :], vt_mx[t], (early_mx[0][:, cols], early_mx[1][:, cols]))
-        ob_bf = sb.tile([P, 2, P * PACK], BF16, name="ob_bf", align_bytes=64)
         for u in range(2):
+            for t in range(PACK):
+                cols = slice((2 * u + 1) * P, (2 * u + 2) * P)
+                mx_pass(nc, o_ps[u][:, t, :], vt_mx[t], (early_mx[0][:, cols], early_mx[1][:, cols]))
+        wo_mx = []
+
+        def wo_quarter(c):
+            wo_bf = sb.tile([P, P * PACK], BF16, name="wo_bf%d" % c, tag="wo_bf%d" % c, align_bytes=64)
+            nc.scalar.copy(
+                out=wo_bf[:].rearrange("p (m i t) -> p m t i", i=4, t=PACK),
+                in_=wo_raw[c // 2][:, :, (c % 2) * P : (c % 2 + 1) * P].rearrange("p t (m i) -> p m t i", i=4),
+            )
+            pair = mx_tiles("wo%d" % c, P)
+            quantize(nc, pair[0][:], pair[1][:], wo_bf[:])
+            wo_mx.append((pair[0][:], pair[1][:]))
+
+        wo_quarter(0)
+        ob_bf = []
+        for u in range(2):
+            ob_bf.append(sb.tile([P, P * PACK], BF16, name="ob_bf%d" % u, tag=("wo_bf0", "ob_bf1")[u], align_bytes=64))
             nc.vector.tensor_tensor(
-                ob_bf[:, u, :].rearrange("p (x j t) -> p x t j", j=4, t=PACK),
+                ob_bf[u][:].rearrange("p (x j t) -> p x t j", j=4, t=PACK),
                 o_ps[u][:].rearrange("p t (x j) -> p x t j", j=4),
                 factor[:].rearrange("p t (x u j) -> p u x t j", u=2, j=4)[:, u],
                 ALU.mult,
             )
-        wo_mx = []
-        for h in range(2):
-            wo_bf = sb.tile([P, (F // 2) * PACK], BF16, name="wo_bf%d" % h, tag="wo_bf%d" % h, align_bytes=64)
-            nc.scalar.copy(
-                out=wo_bf[:].rearrange("p (c m i t) -> p c m t i", c=2, i=2, t=PACK),
-                in_=wo_raw[h][:].rearrange("p t (m i c) -> p c m t i", i=2, c=2),
-            )
-            wo_mx.append(mx_tiles("wo%d" % h, F // 2))
-            quantize(nc, wo_mx[h][0][:], wo_mx[h][1][:], wo_bf[:])
-            if h == 0:
-                ob_mx = mx_tiles("ob", Q)
-                quantize(nc, ob_mx[0][:], ob_mx[1][:], ob_bf[:].rearrange("p u n -> p (u n)"))
+        ob_mx = mx_tiles("ob", Q)
+        for u in range(2):
+            half = slice(u * P, (u + 1) * P)
+            quantize(nc, ob_mx[0][:, half], ob_mx[1][:, half], ob_bf[u][:])
+        for c in range(1, PACK):
+            wo_quarter(c)
 
-        z_sum = sb.tile([P, 2, 2 * X], F32, name="z_sum", tag="wo_bf1", align_bytes=64)
+        out_rows = out.rearrange("(c p) x -> p c x", p=P)
         for h in range(2):
             z_ps = ps.tile([P, 2, P], F32, name="z_ps%d" % h, tag="score%d" % h)
             for c in range(2):
-                cols = slice(c * P, (c + 1) * P)
                 for u in range(2):
                     half = slice(u * P, (u + 1) * P)
                     mx_pass(
                         nc,
                         z_ps[:, c, :],
-                        (wo_mx[h][0][:, cols], wo_mx[h][1][:, cols]),
+                        wo_mx[2 * h + c],
                         (ob_mx[0][:, half], ob_mx[1][:, half]),
                         start=(u == 0),
                         stop=(u == 1),
                     )
-            nc.vector.tensor_reduce(z_sum[:, h, :], z_ps[:].rearrange("p c (x j) -> p (c x) j", j=4), AX.X, ALU.add)
-        y = sb.tile([P, 2, 2 * X], F32, name="y")
-        nc.vector.tensor_tensor(y[:], z_sum[:], res_sb[:], ALU.add)
-        nc.sync.dma_start(out=out.rearrange("(h p c) x -> p h (c x)", h=2, c=2), in_=y[:])
+            z_sum = sb.tile([P, 2 * X], F32, name="z_sum%d" % h, tag=("wo_bf3", "z_sum1")[h], align_bytes=64)
+            nc.vector.tensor_reduce(z_sum[:], z_ps[:].rearrange("p c (x j) -> p (c x) j", j=4), AX.X, ALU.add)
+            y = sb.tile([P, 2, X], F32, name="y%d" % h)
+            nc.vector.tensor_tensor(
+                y[:], z_sum[:].rearrange("p (c x) -> p c x", c=2), res_sb[:, 2 * h : 2 * h + 2, :], ALU.add
+            )
+            (nc.scalar, nc.sync)[h].dma_start(out=out_rows[:, 2 * h : 2 * h + 2, :], in_=y[:])

@@ -18,20 +18,29 @@ AX = mybir.AxisListType
 
 P = 128
 PACK = 4
+RUN = 4
+HEADS_HALF = 4
+GROUP = 16
 CAST_FIRST = 1536
 
 
-def quantize(nc, codes, scales, values):
+def quantize(nc, operand, values):
+    codes, scales = operand
     nc.vector.quantize_mx(out=codes.bitcast(FP8X4), scales=scales, in_=values)
 
 
-def mx_pass(nc, out, lhs, rhs, start=True, stop=True):
+def columns(operand, first, count=1):
+    cols = slice(first * P, (first + count) * P)
+    return operand[0][:, cols], operand[1][:, cols]
+
+
+def mx_pass(nc, result, stationary, moving, start=True, stop=True):
     nc.tensor.matmul_mx(
-        out=out,
-        lhsT=lhs[0].bitcast(FP8X4),
-        lhsT_scale=lhs[1],
-        rhs=rhs[0].bitcast(FP8X4),
-        rhs_scale=rhs[1],
+        out=result,
+        lhsT=stationary[0].bitcast(FP8X4),
+        lhsT_scale=stationary[1],
+        rhs=moving[0].bitcast(FP8X4),
+        rhs_scale=moving[1],
         start=start,
         stop=stop,
     )
@@ -46,9 +55,9 @@ def tile_attend_ownlists_project_kernel(tc, query, keys, size, vals, own, esc, w
         def mx_tiles(name, width, tag=None):
             codes = sb.tile([P, width], U32, name=name + "_codes", tag=tag or name + "_codes", align_bytes=64)
             scales = sb.tile([P, width], U8, name=name + "_scales", align_bytes=64)
-            return codes, scales
+            return codes[:], scales[:]
 
-        lists = sb.tile([P, I // 16], U16, name="lists")
+        lists = sb.tile([P, I // GROUP], U16, name="lists")
         key_planes = keys.rearrange("(p t) n -> t p n", t=PACK)
         val_planes = vals.rearrange("(p t) n -> t p n", t=PACK)
         key_pool = [sb.tile([P, T], F32, name="key_pool%d" % t) for t in range(PACK)]
@@ -65,174 +74,155 @@ def tile_attend_ownlists_project_kernel(tc, query, keys, size, vals, own, esc, w
         nc.sync.dma_start(out=key_pool[0][:], in_=key_planes[0])
         nc.sync.dma_start(lists[:], offs)
         nc.scalar.dma_start(out=size_sb[:], in_=size.rearrange("o (p t) -> p (o t)", t=PACK))
-        nc.scalar.dma_start(out=esc_sb[:], in_=esc.rearrange("(p t) o -> p (t o)", t=PACK))
-        nc.scalar.dma_start(out=res_sb[:], in_=res.rearrange("(c p) x -> p c x", p=P))
         for t in range(1, PACK):
             nc.sync.dma_start(out=key_pool[t][:], in_=key_planes[t])
         nc.sync.dma_start(out=q_raw[:], in_=query.rearrange("(p t) q -> p t q", t=PACK))
         for t in range(PACK):
             nc.sync.dma_start(out=val_pool[t][:], in_=val_planes[t])
+        nc.sync.dma_start(out=esc_sb[:], in_=esc.rearrange("(p t) o -> p (t o)", t=PACK))
         own_rows = own.rearrange("(p t) q -> p t q", t=PACK)
         for h in range(2):
             nc.sync.dma_start(out=own_sb[h][:], in_=own_rows[:, 2 * h : 2 * h + 2, :])
         wo_rows = wo.rearrange("(p t) f -> p t f", t=PACK)
         for h in range(2):
             nc.sync.dma_start(out=wo_raw[h][:], in_=wo_rows[:, :, h * (F // 2) : (h + 1) * (F // 2)])
+        nc.sync.dma_start(out=res_sb[:], in_=res.rearrange("(c p) x -> p c x", p=P))
 
         ident = sb.tile([P, P], F32, name="ident")
         make_identity(nc, ident[:])
 
-        size_ps = ps.tile([P, PACK, P], F32, name="size_ps", tag="size_ps")
+        size_ps = ps.tile([P, PACK, P], F32, name="size_ps")
         for t in range(PACK):
             nc.tensor.transpose(size_ps[:, t, :], size_sb[:, t : t + 1].to_broadcast([P, P]), ident[:])
 
         q_mx = mx_tiles("q", Q)
         for u in range(2):
-            half = slice(u * P, (u + 1) * P)
             q_bf = sb.tile([P, P * PACK], BF16, name="q_bf%d" % u, align_bytes=64)
             nc.scalar.copy(
-                out=q_bf[:].rearrange("p (x j t) -> p x t j", j=4, t=PACK),
-                in_=q_raw[:].rearrange("p t (x u j) -> p u x t j", u=2, j=4)[:, u],
+                out=q_bf[:].rearrange("p (x j t) -> p x t j", j=HEADS_HALF, t=PACK),
+                in_=q_raw[:].rearrange("p t (x u j) -> p u x t j", u=2, j=HEADS_HALF)[:, u],
             )
-            quantize(nc, q_mx[0][:, half], q_mx[1][:, half], q_bf[:])
+            quantize(nc, columns(q_mx, u), q_bf[:])
 
         k_bf = sb.tile([P, I * PACK], BF16, name="k_bf", align_bytes=64)
-        k_places = k_bf[:].rearrange("p (c i u t) -> p u c t i", i=4, u=2, t=2)
-        for u in range(2):
-            k_got = sb.tile([P, 2, I], BF16, name="k_got%d" % u)
+        k_places = k_bf[:].rearrange("p (c i pair t) -> p pair c t i", i=RUN, pair=2, t=2)
+        for pair in range(2):
+            k_got = sb.tile([P, 2, I], BF16, name="k_got%d" % pair)
             for t in range(2):
-                nc.vector.tensor_copy(k_got[:, t, :], key_pool[2 * u + t][:].indirect(lists[:]))
-            nc.vector.tensor_copy(out=k_places[:, u], in_=k_got[:].rearrange("p t (c i) -> p c t i", i=4))
+                nc.vector.tensor_copy(k_got[:, t, :], key_pool[2 * pair + t][:].indirect(lists[:]))
+            nc.vector.tensor_copy(out=k_places[:, pair], in_=k_got[:].rearrange("p t (c i) -> p c t i", i=RUN))
         k_mx = mx_tiles("k", I)
-        quantize(nc, k_mx[0][:], k_mx[1][:], k_bf[:])
+        quantize(nc, k_mx, k_bf[:])
 
-        v_got = {}
-        for t in range(PACK):
-            if t == 0:
-                pool_bf = sb.tile([P, T], BF16, name="pool_bf")
-                nc.scalar.activation(pool_bf[:, :CAST_FIRST], val_pool[0][:, :CAST_FIRST], ACT.Copy)
+        val0_bf = sb.tile([P, T], BF16, name="val0_bf")
+        nc.scalar.activation(val0_bf[:, :CAST_FIRST], val_pool[0][:, :CAST_FIRST], ACT.Copy)
 
-        early_bf = sb.tile([P, 2 * Q * PACK], BF16, name="early_bf", tag="early_bf", align_bytes=64)
-        vt1_bf = sb.tile([P, I], BF16, name="vt1_bf", align_bytes=64)
+        early_bf = sb.tile([P, 4 * I], BF16, name="early_bf", align_bytes=64)
+        vt2_bf = sb.tile([P, I], BF16, name="vt2_bf", align_bytes=64)
 
         def turn(sources, dst, name, bank):
             n = len(sources)
             turned = ps.tile([P, n, 2, P], F32, name="turned_" + name, tag="turn%d" % bank)
             for a in range(n):
                 words = sources[a].bitcast(F32)
-                for u in range(2):
-                    nc.tensor.transpose(turned[:, a, u, :], words[:, u : I // 2 : 2], ident[:])
+                for w in range(2):
+                    nc.tensor.transpose(turned[:, a, w, :], words[:, w : I // 2 : 2], ident[:])
             nc.scalar.copy(
-                out=dst.bitcast(F32).rearrange("p (a e u) -> p a e u", a=n, u=2),
-                in_=turned[:].rearrange("p a u e -> p a e u"),
+                out=dst.bitcast(F32).rearrange("p (a r w) -> p a r w", a=n, w=2),
+                in_=turned[:].rearrange("p a w r -> p a r w"),
             )
 
         total = sb.tile([P, 2], F32, name="total")
         probs = []
-        for g in range(2):
-            cols = slice(g * P, (g + 1) * P)
-            score = ps.tile([P, I], F32, name="score%d" % g, tag="score%d" % g)
-            mx_pass(nc, score[:], (q_mx[0][:, cols], q_mx[1][:, cols]), (k_mx[0][:], k_mx[1][:]))
-            neg_max = sb.tile([P, 1], F32, name="neg_max%d" % g, tag="neg_max%d" % g)
+        for u in range(2):
+            score = ps.tile([P, I], F32, name="score%d" % u, tag="score%d" % u)
+            mx_pass(nc, score[:], columns(q_mx, u), k_mx)
+            neg_max = sb.tile([P, 1], F32, name="neg_max%d" % u, tag="neg_max%d" % u)
             nc.vector.tensor_reduce(neg_max[:], score[:], AX.X, ALU.max, negate=True)
-            prob = sb.tile([P, I], F32, name="prob%d" % g, tag="prob%d" % g)
-            nc.scalar.activation(prob[:], score[:], ACT.Exp, bias=neg_max[:], scale=1.0, accum_out=total[:, g : g + 1])
+            prob = sb.tile([P, I], F32, name="prob%d" % u)
+            nc.scalar.activation(prob[:], score[:], ACT.Exp, bias=neg_max[:], scale=1.0, accum_out=total[:, u : u + 1])
             probs.append(prob)
+        v_got = {}
         for t in range(1, PACK):
             v_got[t] = sb.tile([P, I], BF16, name="v_got%d" % t)
             nc.vector.tensor_copy(v_got[t][:], val_pool[t][:].indirect(lists[:]))
         inv = sb.tile([P, 2], F32, name="inv", tag="val_pool1", align_bytes=64)
         nc.vector.reciprocal(inv[:], total[:])
         weights = []
-        for g in range(2):
-            prob = probs[g]
-            w_bf = sb.tile([P, I], BF16, name="w_bf%d" % g)
+        for u in range(2):
+            w_bf = sb.tile([P, I], BF16, name="w_bf%d" % u)
             nc.vector.scalar_tensor_tensor(
                 w_bf[:].rearrange("p (s t) -> p s t", t=PACK),
-                prob[:].rearrange("p (s t) -> p s t", t=PACK),
-                inv[:, g : g + 1],
+                probs[u][:].rearrange("p (s t) -> p s t", t=PACK),
+                inv[:, u : u + 1],
                 size_ps[:].rearrange("p t s -> p s t"),
                 ALU.mult,
                 ALU.mult,
             )
             weights.append(w_bf[:])
         turn([v_got[1][:], weights[0]], early_bf[:, : 2 * I], "v1w0", 0)
-        nc.scalar.activation(pool_bf[:, CAST_FIRST:], val_pool[0][:, CAST_FIRST:], ACT.Copy)
+        nc.scalar.activation(val0_bf[:, CAST_FIRST:], val_pool[0][:, CAST_FIRST:], ACT.Copy)
         v_got[0] = sb.tile([P, I], BF16, name="v_got0", tag="neg_max1")
-        nc.scalar.activation(v_got[0][:], pool_bf[:].indirect(lists[:]), ACT.Copy)
+        nc.scalar.activation(v_got[0][:], val0_bf[:].indirect(lists[:]), ACT.Copy)
         turn([v_got[0][:], weights[1]], early_bf[:, 2 * I :], "v0w1", 1)
 
         early_mx = mx_tiles("early", 5 * P, tag="val_pool3")
-        quantize(nc, early_mx[0][:, : 4 * P], early_mx[1][:, : 4 * P], early_bf[:])
+        quantize(nc, columns(early_mx, 0, 4), early_bf[:])
         factor = sb.tile([P, PACK, Q], F32, name="factor")
-        turn([v_got[2][:]], vt1_bf[:], "v2", 2)
-        quantize(nc, early_mx[0][:, 4 * P :], early_mx[1][:, 4 * P :], vt1_bf[:])
-        for r in range(2):
-            nc.scalar.activation(factor[:, r, :], own_sb[0][:, r, :], ACT.Copy, scale=esc_sb[:, r : r + 1])
-            nc.vector.tensor_scalar_mul(factor[:, 2 + r, :], own_sb[1][:, r, :], esc_sb[:, 2 + r : 3 + r])
+        turn([v_got[2][:]], vt2_bf[:], "v2", 2)
+        quantize(nc, columns(early_mx, 4), vt2_bf[:])
+        for t in range(2):
+            nc.scalar.activation(factor[:, t, :], own_sb[0][:, t, :], ACT.Copy, scale=esc_sb[:, t : t + 1])
+            nc.vector.tensor_scalar_mul(factor[:, 2 + t, :], own_sb[1][:, t, :], esc_sb[:, 2 + t : 3 + t])
         vt3_bf = sb.tile([P, I], BF16, name="vt3_bf", tag="own_sb0", align_bytes=64)
         turn([v_got[3][:]], vt3_bf[:], "v3", 0)
         vt3_mx = mx_tiles("vt3", P)
-        quantize(nc, vt3_mx[0][:], vt3_mx[1][:], vt3_bf[:])
-        vt_mx = [
-            (early_mx[0][:, 2 * P : 3 * P], early_mx[1][:, 2 * P : 3 * P]),
-            (early_mx[0][:, :P], early_mx[1][:, :P]),
-            (early_mx[0][:, 4 * P :], early_mx[1][:, 4 * P :]),
-            (vt3_mx[0][:], vt3_mx[1][:]),
-        ]
+        quantize(nc, vt3_mx, vt3_bf[:])
+        vt_mx = [columns(early_mx, 2), columns(early_mx, 0), columns(early_mx, 4), vt3_mx]
+        wt_mx = [columns(early_mx, 1), columns(early_mx, 3)]
 
         o_ps = [ps.tile([P, PACK, P], F32, name="o_ps%d" % u) for u in range(2)]
         for u in range(2):
             for t in range(PACK):
-                cols = slice((2 * u + 1) * P, (2 * u + 2) * P)
-                mx_pass(nc, o_ps[u][:, t, :], vt_mx[t], (early_mx[0][:, cols], early_mx[1][:, cols]))
+                mx_pass(nc, o_ps[u][:, t, :], vt_mx[t], wt_mx[u])
+
         wo_mx = []
 
-        def wo_quarter(c):
+        def wo_block(c):
             wo_bf = sb.tile([P, P * PACK], BF16, name="wo_bf%d" % c, tag="wo_bf%d" % c, align_bytes=64)
             nc.scalar.copy(
-                out=wo_bf[:].rearrange("p (m i t) -> p m t i", i=4, t=PACK),
-                in_=wo_raw[c // 2][:, :, (c % 2) * P : (c % 2 + 1) * P].rearrange("p t (m i) -> p m t i", i=4),
+                out=wo_bf[:].rearrange("p (m i t) -> p m t i", i=RUN, t=PACK),
+                in_=wo_raw[c // 2][:, :, (c % 2) * P : (c % 2 + 1) * P].rearrange("p t (m i) -> p m t i", i=RUN),
             )
-            pair = mx_tiles("wo%d" % c, P)
-            quantize(nc, pair[0][:], pair[1][:], wo_bf[:])
-            wo_mx.append((pair[0][:], pair[1][:]))
+            wo_mx.append(mx_tiles("wo%d" % c, P))
+            quantize(nc, wo_mx[c], wo_bf[:])
 
-        wo_quarter(0)
+        wo_block(0)
         ob_bf = []
         for u in range(2):
             ob_bf.append(sb.tile([P, P * PACK], BF16, name="ob_bf%d" % u, tag=("wo_bf0", "ob_bf1")[u], align_bytes=64))
             nc.vector.tensor_tensor(
-                ob_bf[u][:].rearrange("p (x j t) -> p x t j", j=4, t=PACK),
-                o_ps[u][:].rearrange("p t (x j) -> p x t j", j=4),
-                factor[:].rearrange("p t (x u j) -> p u x t j", u=2, j=4)[:, u],
+                ob_bf[u][:].rearrange("p (x j t) -> p x t j", j=HEADS_HALF, t=PACK),
+                o_ps[u][:].rearrange("p t (x j) -> p x t j", j=HEADS_HALF),
+                factor[:].rearrange("p t (x u j) -> p u x t j", u=2, j=HEADS_HALF)[:, u],
                 ALU.mult,
             )
         ob_mx = mx_tiles("ob", Q)
         for u in range(2):
-            half = slice(u * P, (u + 1) * P)
-            quantize(nc, ob_mx[0][:, half], ob_mx[1][:, half], ob_bf[u][:])
+            quantize(nc, columns(ob_mx, u), ob_bf[u][:])
         for c in range(1, PACK):
-            wo_quarter(c)
+            wo_block(c)
 
         out_rows = out.rearrange("(c p) x -> p c x", p=P)
         for h in range(2):
             z_ps = ps.tile([P, 2, P], F32, name="z_ps%d" % h, tag="score%d" % h)
-            for c in range(2):
+            for b in range(2):
                 for u in range(2):
-                    half = slice(u * P, (u + 1) * P)
-                    mx_pass(
-                        nc,
-                        z_ps[:, c, :],
-                        wo_mx[2 * h + c],
-                        (ob_mx[0][:, half], ob_mx[1][:, half]),
-                        start=(u == 0),
-                        stop=(u == 1),
-                    )
+                    mx_pass(nc, z_ps[:, b, :], wo_mx[2 * h + b], columns(ob_mx, u), start=(u == 0), stop=(u == 1))
             z_sum = sb.tile([P, 2 * X], F32, name="z_sum%d" % h, tag=("wo_bf3", "z_sum1")[h], align_bytes=64)
-            nc.vector.tensor_reduce(z_sum[:], z_ps[:].rearrange("p c (x j) -> p (c x) j", j=4), AX.X, ALU.add)
+            nc.vector.tensor_reduce(z_sum[:], z_ps[:].rearrange("p b (x j) -> p (b x) j", j=HEADS_HALF), AX.X, ALU.add)
             y = sb.tile([P, 2, X], F32, name="y%d" % h)
             nc.vector.tensor_tensor(
-                y[:], z_sum[:].rearrange("p (c x) -> p c x", c=2), res_sb[:, 2 * h : 2 * h + 2, :], ALU.add
+                y[:], z_sum[:].rearrange("p (b x) -> p b x", b=2), res_sb[:, 2 * h : 2 * h + 2, :], ALU.add
             )
             (nc.scalar, nc.sync)[h].dma_start(out=out_rows[:, 2 * h : 2 * h + 2, :], in_=y[:])

from contextlib import ExitStack

import concourse.mybir as mybir
from concourse.masks import make_identity

D, T, I, Q, X, E, F = 512, 2048, 512, 256, 32, 512, 512
FLOPS = 2 * Q * I * D + 2 * E * Q * I + 2 * F * Q * E

F32 = mybir.dt.float32
BF16 = mybir.dt.bfloat16
U32 = mybir.dt.uint32
U16 = mybir.dt.uint16
U8 = mybir.dt.uint8
FP8X4 = mybir.dt.float8_e4m3fn_x4
ALU = mybir.AluOpType
ACT = mybir.ActivationFunctionType
AX = mybir.AxisListType

P = 128
PACK = 4
RUN = 4
HEADS_HALF = 4
GROUP = 16
CAST_FIRST = 1536


def quantize(nc, operand, values):
    codes, scales = operand
    nc.vector.quantize_mx(out=codes.bitcast(FP8X4), scales=scales, in_=values)


def columns(operand, first, count=1):
    cols = slice(first * P, (first + count) * P)
    return operand[0][:, cols], operand[1][:, cols]


def mx_pass(nc, result, stationary, moving, start=True, stop=True):
    nc.tensor.matmul_mx(
        out=result,
        lhsT=stationary[0].bitcast(FP8X4),
        lhsT_scale=stationary[1],
        rhs=moving[0].bitcast(FP8X4),
        rhs_scale=moving[1],
        start=start,
        stop=stop,
    )


def tile_attend_ownlists_project_kernel(tc, query, keys, size, vals, own, esc, wo, res, offs, out):
    nc = tc.nc
    with ExitStack() as ctx:
        sb = ctx.enter_context(tc.tile_pool(name="sb", bufs=1))
        ps = ctx.enter_context(tc.psum_pool(name="ps", bufs=1))

        def mx_tiles(name, width, tag=None):
            codes = sb.tile([P, width], U32, name=name + "_codes", tag=tag or name + "_codes", align_bytes=64)
            scales = sb.tile([P, width], U8, name=name + "_scales", align_bytes=64)
            return codes[:], scales[:]

        lists = sb.tile([P, I // GROUP], U16, name="lists")
        key_planes = keys.rearrange("(p t) n -> t p n", t=PACK)
        val_planes = vals.rearrange("(p t) n -> t p n", t=PACK)
        key_pool = [sb.tile([P, T], F32, name="key_pool%d" % t) for t in range(PACK)]
        val_pool = [
            sb.tile([P, T], F32, name="val_pool%d" % t, tag="val_pool%d" % t, align_bytes=64) for t in range(PACK)
        ]
        q_raw = sb.tile([P, PACK, Q], F32, name="q_raw")
        own_sb = [sb.tile([P, 2, Q], F32, name="own_sb%d" % h, tag="own_sb%d" % h, align_bytes=64) for h in range(2)]
        wo_raw = [sb.tile([P, PACK, F // 2], F32, name="wo_raw%d" % h) for h in range(2)]
        size_sb = sb.tile([P, PACK], F32, name="size_sb")
        esc_sb = sb.tile([P, PACK], F32, name="esc_sb")
        res_sb = sb.tile([P, PACK, X], F32, name="res_sb")

        nc.sync.dma_start(out=key_pool[0][:], in_=key_planes[0])
        nc.sync.dma_start(lists[:], offs)
        nc.scalar.dma_start(out=size_sb[:], in_=size.rearrange("o (p t) -> p (o t)", t=PACK))
        for t in range(1, PACK):
            nc.sync.dma_start(out=key_pool[t][:], in_=key_planes[t])
        nc.sync.dma_start(out=q_raw[:], in_=query.rearrange("(p t) q -> p t q", t=PACK))
        for t in range(PACK):
            nc.sync.dma_start(out=val_pool[t][:], in_=val_planes[t])
        nc.sync.dma_start(out=esc_sb[:], in_=esc.rearrange("(p t) o -> p (t o)", t=PACK))
        own_rows = own.rearrange("(p t) q -> p t q", t=PACK)
        for h in range(2):
            nc.sync.dma_start(out=own_sb[h][:], in_=own_rows[:, 2 * h : 2 * h + 2, :])
        wo_rows = wo.rearrange("(p t) f -> p t f", t=PACK)
        for h in range(2):
            nc.sync.dma_start(out=wo_raw[h][:], in_=wo_rows[:, :, h * (F // 2) : (h + 1) * (F // 2)])
        nc.sync.dma_start(out=res_sb[:], in_=res.rearrange("(c p) x -> p c x", p=P))

        ident = sb.tile([P, P], F32, name="ident")
        make_identity(nc, ident[:])

        size_ps = ps.tile([P, PACK, P], F32, name="size_ps")
        for t in range(PACK):
            nc.tensor.transpose(size_ps[:, t, :], size_sb[:, t : t + 1].to_broadcast([P, P]), ident[:])

        q_mx = mx_tiles("q", Q)
        for u in range(2):
            q_bf = sb.tile([P, P * PACK], BF16, name="q_bf%d" % u, align_bytes=64)
            nc.scalar.copy(
                out=q_bf[:].rearrange("p (x j t) -> p x t j", j=HEADS_HALF, t=PACK),
                in_=q_raw[:].rearrange("p t (x u j) -> p u x t j", u=2, j=HEADS_HALF)[:, u],
            )
            quantize(nc, columns(q_mx, u), q_bf[:])

        k_bf = sb.tile([P, I * PACK], BF16, name="k_bf", align_bytes=64)
        k_places = k_bf[:].rearrange("p (c i pair t) -> p pair c t i", i=RUN, pair=2, t=2)
        for pair in range(2):
            k_got = sb.tile([P, 2, I], BF16, name="k_got%d" % pair)
            for t in range(2):
                nc.vector.tensor_copy(k_got[:, t, :], key_pool[2 * pair + t][:].indirect(lists[:]))
            nc.vector.tensor_copy(out=k_places[:, pair], in_=k_got[:].rearrange("p t (c i) -> p c t i", i=RUN))
        k_mx = mx_tiles("k", I)
        quantize(nc, k_mx, k_bf[:])

        val0_bf = sb.tile([P, T], BF16, name="val0_bf")
        nc.scalar.activation(val0_bf[:, :CAST_FIRST], val_pool[0][:, :CAST_FIRST], ACT.Copy)

        early_bf = sb.tile([P, 4 * I], BF16, name="early_bf", align_bytes=64)
        vt2_bf = sb.tile([P, I], BF16, name="vt2_bf", align_bytes=64)

        def turn(sources, dst, name, bank):
            n = len(sources)
            turned = ps.tile([P, n, 2, P], F32, name="turned_" + name, tag="turn%d" % bank)
            for a in range(n):
                words = sources[a].bitcast(F32)
                for w in range(2):
                    nc.tensor.transpose(turned[:, a, w, :], words[:, w : I // 2 : 2], ident[:])
            nc.scalar.copy(
                out=dst.bitcast(F32).rearrange("p (a r w) -> p a r w", a=n, w=2),
                in_=turned[:].rearrange("p a w r -> p a r w"),
            )

        total = sb.tile([P, 2], F32, name="total")
        probs = []
        for u in range(2):
            score = ps.tile([P, I], F32, name="score%d" % u, tag="score%d" % u)
            mx_pass(nc, score[:], columns(q_mx, u), k_mx)
            neg_max = sb.tile([P, 1], F32, name="neg_max%d" % u, tag="neg_max%d" % u)
            nc.vector.tensor_reduce(neg_max[:], score[:], AX.X, ALU.max, negate=True)
            prob = sb.tile([P, I], F32, name="prob%d" % u)
            nc.scalar.activation(prob[:], score[:], ACT.Exp, bias=neg_max[:], scale=1.0, accum_out=total[:, u : u + 1])
            probs.append(prob)
        v_got = {}
        for t in range(1, PACK):
            v_got[t] = sb.tile([P, I], BF16, name="v_got%d" % t)
            nc.vector.tensor_copy(v_got[t][:], val_pool[t][:].indirect(lists[:]))
        inv = sb.tile([P, 2], F32, name="inv", tag="val_pool1", align_bytes=64)
        nc.vector.reciprocal(inv[:], total[:])
        weights = []
        for u in range(2):
            w_bf = sb.tile([P, I], BF16, name="w_bf%d" % u)
            nc.vector.scalar_tensor_tensor(
                w_bf[:].rearrange("p (s t) -> p s t", t=PACK),
                probs[u][:].rearrange("p (s t) -> p s t", t=PACK),
                inv[:, u : u + 1],
                size_ps[:].rearrange("p t s -> p s t"),
                ALU.mult,
                ALU.mult,
            )
            weights.append(w_bf[:])
        turn([v_got[1][:], weights[0]], early_bf[:, : 2 * I], "v1w0", 0)
        nc.scalar.activation(val0_bf[:, CAST_FIRST:], val_pool[0][:, CAST_FIRST:], ACT.Copy)
        v_got[0] = sb.tile([P, I], BF16, name="v_got0", tag="neg_max1")
        nc.scalar.activation(v_got[0][:], val0_bf[:].indirect(lists[:]), ACT.Copy)
        turn([v_got[0][:], weights[1]], early_bf[:, 2 * I :], "v0w1", 1)

        early_mx = mx_tiles("early", 5 * P, tag="val_pool3")
        quantize(nc, columns(early_mx, 0, 4), early_bf[:])
        factor = sb.tile([P, PACK, Q], F32, name="factor")
        turn([v_got[2][:]], vt2_bf[:], "v2", 2)
        quantize(nc, columns(early_mx, 4), vt2_bf[:])
        for t in range(2):
            nc.scalar.activation(factor[:, t, :], own_sb[0][:, t, :], ACT.Copy, scale=esc_sb[:, t : t + 1])
            nc.vector.tensor_scalar_mul(factor[:, 2 + t, :], own_sb[1][:, t, :], esc_sb[:, 2 + t : 3 + t])
        vt3_bf = sb.tile([P, I], BF16, name="vt3_bf", tag="own_sb0", align_bytes=64)
        turn([v_got[3][:]], vt3_bf[:], "v3", 0)
        vt3_mx = mx_tiles("vt3", P)
        quantize(nc, vt3_mx, vt3_bf[:])
        vt_mx = [columns(early_mx, 2), columns(early_mx, 0), columns(early_mx, 4), vt3_mx]
        wt_mx = [columns(early_mx, 1), columns(early_mx, 3)]

        o_ps = [ps.tile([P, PACK, P], F32, name="o_ps%d" % u) for u in range(2)]
        for u in range(2):
            for t in range(PACK):
                mx_pass(nc, o_ps[u][:, t, :], vt_mx[t], wt_mx[u])

        wo_mx = []

        def wo_block(c):
            wo_bf = sb.tile([P, P * PACK], BF16, name="wo_bf%d" % c, tag="wo_bf%d" % c, align_bytes=64)
            nc.scalar.copy(
                out=wo_bf[:].rearrange("p (m i t) -> p m t i", i=RUN, t=PACK),
                in_=wo_raw[c // 2][:, :, (c % 2) * P : (c % 2 + 1) * P].rearrange("p t (m i) -> p m t i", i=RUN),
            )
            wo_mx.append(mx_tiles("wo%d" % c, P))
            quantize(nc, wo_mx[c], wo_bf[:])

        wo_block(0)
        ob_bf = []
        for u in range(2):
            ob_bf.append(sb.tile([P, P * PACK], BF16, name="ob_bf%d" % u, tag=("wo_bf0", "ob_bf1")[u], align_bytes=64))
            nc.vector.tensor_tensor(
                ob_bf[u][:].rearrange("p (x j t) -> p x t j", j=HEADS_HALF, t=PACK),
                o_ps[u][:].rearrange("p t (x j) -> p x t j", j=HEADS_HALF),
                factor[:].rearrange("p t (x u j) -> p u x t j", u=2, j=HEADS_HALF)[:, u],
                ALU.mult,
            )
        ob_mx = mx_tiles("ob", Q)
        for u in range(2):
            quantize(nc, columns(ob_mx, u), ob_bf[u][:])
        for c in range(1, PACK):
            wo_block(c)

        out_rows = out.rearrange("(c p) x -> p c x", p=P)
        for h in range(2):
            z_ps = ps.tile([P, 2, P], F32, name="z_ps%d" % h, tag="score%d" % h)
            for b in range(2):
                for u in range(2):
                    mx_pass(nc, z_ps[:, b, :], wo_mx[2 * h + b], columns(ob_mx, u), start=(u == 0), stop=(u == 1))
            z_sum = sb.tile([P, 2 * X], F32, name="z_sum%d" % h, tag=("wo_bf3", "z_sum1")[h], align_bytes=64)
            nc.vector.tensor_reduce(z_sum[:], z_ps[:].rearrange("p b (x j) -> p (b x) j", j=HEADS_HALF), AX.X, ALU.add)
            y = sb.tile([P, 2, X], F32, name="y%d" % h)
            nc.vector.tensor_tensor(
                y[:], z_sum[:].rearrange("p (b x) -> p b x", b=2), res_sb[:, 2 * h : 2 * h + 2, :], ALU.add
            )
            (nc.scalar, nc.sync)[h].dma_start(out=out_rows[:, 2 * h : 2 * h + 2, :], in_=y[:])
